import numpy as np, ml_dtypes
CORES = [36,164,52,180,100,228,116,244]
N = 8
import mx_ref
NC, G = 128, 4
C = np.float32(0.043)
BF = ml_dtypes.bfloat16
def cut(t, i, w=512):
    return t[:, w * i:w * i + w]
def tile(rs):
    return np.stack(rs, axis=2).reshape(128, -1).astype(BF)
def layer(w, X):
    out = []
    for i in range(G):
        for t in range(len(X)):
            p = mx_ref.matmul(mx_ref.quantize(cut(w, len(X) * i + t)), X[t])
            z = p if t == 0 else z + p
        out.append(z)
    return out
def act(Z):
    return [np.maximum(z, 0) * C for z in Z]
def setup_inputs(rng):
    def f(*shape):
        return mx_ref.flush((rng.standard_normal(shape, dtype=np.float32) * np.exp2(rng.integers(-2, 3, shape[:-1] + (1,)))).astype(BF))
    return {"x": f(N, 128, 4 * NC), "w1": f(N, 128, G * 512), "w2": f(N, 128, 512)}
def setup_inputs_blocks(rng):
    d = setup_inputs(rng)
    for k in ("x", "w1", "w2"): d[k] = mx_ref.spread(d[k], rng, 4)
    return d
def setup_inputs_wide(rng):
    d = setup_inputs(rng)
    for k in ("x", "w1", "w2"): d[k] = mx_ref.flush((d[k].astype(np.float32) * np.exp2(rng.integers(-8, 9, (N, 1, 1))).astype(np.float32)).astype(BF))
    return d
def setup_inputs_zeros(rng):
    d = setup_inputs(rng); v = d["x"].reshape(N, 128, -1, 4).copy()
    v[np.broadcast_to((rng.random((N, 1, v.shape[2], 1)) < 0.33), v.shape)] = 0
    d["x"] = v.reshape(d["x"].shape)
    return d
def reference(x, w1, w2):
    H = [mx_ref.quantize(tile(act(layer(w1[j], [mx_ref.quantize(x[j])])))) for j in range(N)]
    y = np.full((N, 128, N * NC), np.nan, np.float32)
    for r in range(N):
        qw = mx_ref.quantize(w2[r])
        for j in range(r + 1):
            y[r][:, NC * j:NC * j + NC] = mx_ref.matmul(qw, H[j])
    return {"y": y}

from concourse.bass import DstId, RemoteDMATransfer
from concourse.mybir import dt, AluOpType, ActivationFunctionType

N = 8
NC = 128
TW = 512
G = 4
C = 0.043
BANK = 512
LONG = 3
LANES = [(None, [1, 2, 3, 4]), (True, [5, 6]), (True, [7])]
PLANE_FIRST = True

SCRATCH = {
    "xb": ("sbuf", [128, TW], "bfloat16"),
    "w1b": ("sbuf", [128, G * TW], "bfloat16"),
    "w2b": ("sbuf", [128, TW], "bfloat16"),
    "xq": ("sbuf", [128, NC], "float8_e4m3fn_x4"),
    "xs": ("sbuf", [128, NC], "uint8"),
    "w1q": ("sbuf", [128, G * NC], "float8_e4m3fn_x4"),
    "w1s": ("sbuf", [128, G * NC], "uint8"),
    "w2q": ("sbuf", [128, NC], "float8_e4m3fn_x4"),
    "w2s": ("sbuf", [128, NC], "uint8"),
    "h": ("sbuf", [128, TW], "bfloat16"),
    "hq": ("sbuf", [128, N * NC], "float8_e4m3fn_x4"),
    "hs": ("sbuf", [128, N * NC], "uint8"),
    "yb": ("sbuf", [128, N * NC], "float32"),
    "zp": ("psum", [128, G * BANK], "float32"),
    "yp": ("psum", [128, G * BANK], "float32"),
}
SEMAPHORES = (["ldx", "ldwa", "ldwb", "ldw2", "qx", "act", "hq", "qlast", "st", "sent", "sds", "sdc"]
              + ["qw%d" % i for i in range(G)] + ["mm%d" % i for i in range(G)]
              + ["arr%d" % j for j in range(N)] + ["ym%d" % k for k in range(N)] + ["cp%d" % k for k in range(N)])


def _engines(mask):
    return bin(mask).count("1")


def _mask(topo, core, cores):
    mask = topo.mask(core, cores[0])
    for d in cores[1:]:
        mask &= topo.mask(core, d)
    return mask


def _plan(T, topo):
    plan = []
    for j in range(N):
        src = T.cores[j]
        span = topo.CORES_PER_CHIP
        chip = [c for c in range(max(0, src - span + 1), src + span)
                if c != src and T.rank_of(c) is None and topo.may_write(src, c)
                and topo.host(c) == topo.host(src) and topo.chip(c) == topo.chip(src)]
        lanes = []
        for other, dists in LANES:
            served = [j + d for d in dists if j + d < N]
            if other is None:
                lanes.append((src, served))
            elif served:
                taken = [c for c, _ in lanes]
                free = [c for c in chip if c not in taken and (topo.die(c) != topo.die(src)) == other
                        and all(topo.may_write(c, T.cores[r]) for r in served)]
                lanes.append((free[0], served))
        plan.append(lanes)
    return plan


def _hand_mask(T, topo, lanes):
    src, served = lanes[0]
    return _mask(topo, src, [c for c, _ in lanes[1:]]) & ~_mask(topo, src, [T.cores[r] for r in served])


def _expected(r, plan):
    keys = []
    for j in range(r):
        for i, (sender, served) in enumerate(plan[j]):
            if r in served:
                keys.append(((min(i, 1), served.index(r), i), j, sender, served))
    return sorted(keys)


def _block(T, j, plane):
    if plane:
        return T.hs[:, NC * j:NC * (j + 1)]
    return T.hq[:, NC * j:NC * (j + 1)].bitcast(dt.uint8)


def _send(g, T, topo, core, j, plane, parts):
    transfers = []
    for mask, sem, cores in parts:
        ids = []
        for d in cores:
            rid, pid = topo.addr(d, core)
            ids.append(DstId(rid=rid, pnc=pid))
        transfers.append(RemoteDMATransfer(dst_ids=ids, dma_engine_mask=mask, remote_sem=sem,
                                           srcs=[_block(T, j, plane)], dsts=[_block(T, j, plane) for _ in cores]))
    g.remote_dma_fused(transfers, local_sem=T.sem.sent)
    return sum(_engines(mask) for mask, _, _ in parts)


def _relay_program(g, core, T, topo, j, lanes, served):
    S = T.sem
    cores = [T.cores[r] for r in served]
    handed = _engines(_hand_mask(T, topo, lanes))
    out = _mask(topo, core, cores)
    left = 0
    for plane in (PLANE_FIRST, not PLANE_FIRST):
        g.wait_ge(S.sds if plane else S.sdc, handed)
        left += _send(g, T, topo, core, j, plane, [(out, S["arr%d" % j], cores)])
    g.wait_ge(S.sent, left)


def rank_program(g, core, T, topo):
    S = T.sem
    plan = _plan(T, topo)
    rank = T.rank_of(core)
    if rank is None:
        for j in range(N):
            for relay, served in plan[j][1:]:
                if relay == core:
                    _relay_program(g, core, T, topo, j, plan[j], served)
        return
    sy, sc, ve, te = g.sync, g.scalar, g.vector, g.tensor
    cut = LONG * TW

    sy.dma_start(T.xb[:], T.x[:]).then_inc(S.ldx, 16)
    sc.dma_start(T.w1b[:, 0:cut], T.w1[:, 0:cut]).then_inc(S.ldwa, 16)
    sy.dma_start(T.w1b[:, cut:G * TW], T.w1[:, cut:G * TW]).then_inc(S.ldwb, 16)
    sy.dma_start(T.w2b[:], T.w2[:]).then_inc(S.ldw2, 16)

    ve.wait_ge(S.ldx, 16)
    ve.quantize_mx(T.xq[:], T.xs[:], T.xb[:]).then_inc(S.qx, 1)
    te.wait_ge(S.qx, 1)
    for i in range(G):
        if i == 0:
            ve.wait_ge(S.ldwa, 16)
        if i == LONG:
            ve.wait_ge(S.ldwb, 16)
        ve.quantize_mx(T.w1q[:, NC * i:NC * (i + 1)], T.w1s[:, NC * i:NC * (i + 1)],
                       T.w1b[:, TW * i:TW * (i + 1)]).then_inc(S["qw%d" % i], 1)
        te.wait_ge(S["qw%d" % i], 1)
        te.matmul_mx(T.zp[:, BANK * i:BANK * i + NC], T.w1q[:, NC * i:NC * (i + 1)], T.w1s[:, NC * i:NC * (i + 1)],
                     T.xq[:], T.xs[:], True, True).then_inc(S["mm%d" % i], 1)
        if i < G - 1:
            sc.wait_ge(S["mm%d" % i], 1)
            sc.activation(T.h[:, i:TW:G], T.zp[:, BANK * i:BANK * i + NC], ActivationFunctionType.Relu,
                          scale=C).then_inc(S.act, 1)
        else:
            ve.wait_ge(S["mm%d" % i], 1)
            ve.tensor_scalar(T.h[:, i:TW:G], T.zp[:, BANK * i:BANK * i + NC], 0.0, C,
                             AluOpType.max, AluOpType.mult).then_inc(S.act, 1)
    ve.wait_ge(S.act, G)
    ve.quantize_mx(T.hq[:, NC * rank:NC * (rank + 1)], T.hs[:, NC * rank:NC * (rank + 1)], T.h[:]).then_inc(S.hq, 1)
    ve.wait_ge(S.ldw2, 16)
    ve.quantize_mx(T.w2q[:], T.w2s[:], T.w2b[:]).then_inc(S.qlast, 1)

    lanes = plan[rank]
    if lanes[0][1]:
        direct = [T.cores[r] for r in lanes[0][1]]
        g.wait_ge(S.hq, 1)
        left = 0
        for plane in (PLANE_FIRST, not PLANE_FIRST):
            parts = []
            if lanes[1:]:
                parts.append((_hand_mask(T, topo, lanes), S.sds if plane else S.sdc, [c for c, _ in lanes[1:]]))
            parts.append((_mask(topo, core, direct), S["arr%d" % rank], direct))
            left += _send(g, T, topo, core, rank, plane, parts)
        g.wait_ge(S.sent, left)

    order = [rank]
    te.wait_ge(S.hq, 1)
    te.wait_ge(S.qlast, 1)
    for k, (j, full) in enumerate([(rank, 0)] + [(j, 2 * _engines(_mask(topo, sender, [T.cores[r] for r in served])))
                                                 for _, j, sender, served in _expected(rank, plan)]):
        bank = (T.yp if k < G else T.zp)[:, BANK * (k % G):BANK * (k % G) + NC]
        if j != rank:
            order.append(j)
            te.wait_ge(S["arr%d" % j], full)
        te.matmul_mx(bank, T.w2q[:], T.w2s[:], T.hq[:, NC * j:NC * (j + 1)], T.hs[:, NC * j:NC * (j + 1)],
                     True, True).then_inc(S["ym%d" % k], 1)
        if k % 2 == 0:
            ve.wait_ge(S["ym%d" % k], 1)
            ve.tensor_copy(T.yb[:, NC * j:NC * (j + 1)], bank).then_inc(S["cp%d" % k], 1)
        else:
            sc.wait_ge(S["ym%d" % k], 1)
            sc.activation(T.yb[:, NC * j:NC * (j + 1)], bank, ActivationFunctionType.Copy).then_inc(S["cp%d" % k], 1)
    groups = [[k] for k in range(len(order))]
    if len(order) > 1 and order[1] == rank - 1:
        groups = [[0, 1]] + groups[2:]
    for group in groups:
        for k in group:
            sy.wait_ge(S["cp%d" % k], 1)
        lo = NC * min(order[k] for k in group)
        hi = NC * (max(order[k] for k in group) + 1)
        sy.dma_start(T.y[:, lo:hi], T.yb[:, lo:hi]).then_inc(S.st, 16)
    sy.wait_ge(S.st, 16 * len(groups))
